import numpy as np
import ml_dtypes


def mxq(x, axis, fmt="e4m3"):
    dtype, down = {"e4m3": (ml_dtypes.float8_e4m3fn, 7), "e5m2": (ml_dtypes.float8_e5m2, 14)}[fmt]
    v = np.moveaxis(np.asarray(x, np.float32).astype(ml_dtypes.bfloat16).astype(np.float64), axis, -1)
    blocks = v.reshape(v.shape[:-1] + (-1, 32))
    amax = np.abs(blocks).max(-1, keepdims=True)
    byte = np.maximum(np.where(amax > 0, np.frexp(amax)[1] - 1 + 127, 0) - down, 1)
    scale = np.exp2(byte - 127.0)
    codes = (blocks / scale).astype(np.float32).astype(dtype).astype(np.float64)
    return np.moveaxis((codes * scale).reshape(v.shape), -1, axis)


WIDE = False


def mx_kscale(k):
    if not WIDE:
        return np.ones(k)
    levels = np.array([10, -10, 5, -5, 0])
    if k % 512:
        return np.exp2(np.random.permutation(np.resize(levels, k // 32))).repeat(32)
    a = np.empty((k // 512, 16))
    for p in range(k // 512):
        a[p, :8] = np.random.permutation(np.resize(levels, 8))
        for g in range(8):
            far = levels[np.abs(levels - a[p, g]) >= 10]
            a[p, g + 8] = far[np.random.randint(len(far))]
    return np.exp2(a.ravel()).repeat(32)


def f64(x):
    return np.asarray(x).astype(np.float64)


def striped(idx):
    return np.tile(idx.reshape(-1, 16).T, (8, 1)).astype(np.uint16)


def unstriped(offs):
    return offs[:16].T.reshape(-1).astype(np.int64)


def pack_weight(w):
    k, n = w.shape
    w = f64(np.asarray(w, np.float32).astype(ml_dtypes.bfloat16)).reshape(k // 32, 32, n)
    amax = np.abs(w).max(1)
    byte = np.clip(np.where(amax > 0, np.frexp(amax)[1] - 1 + 127 - 7, 1), 1, 254)
    scaled = (w * np.exp2(127.0 - byte)[:, None, :]).reshape(k, n).astype(np.float32)
    words = np.ascontiguousarray(scaled.reshape(k // 512, 128, 4, n).transpose(0, 1, 3, 2)).astype(ml_dtypes.float8_e4m3fn).view(np.uint8)
    return words, np.ascontiguousarray(byte.astype(np.uint8).reshape(k // 512, 16, n))


def unpack_weight(words, scales):
    g, p, n, _ = words.shape
    vals = np.ascontiguousarray(words).view(ml_dtypes.float8_e4m3fn).astype(np.float64) * np.repeat(np.exp2(scales.astype(np.float64) - 127.0), 8, axis=1)[..., None]
    return vals.transpose(0, 1, 3, 2).reshape(g * 512, n)


def relu(v):
    return np.maximum(v, 0.0)


def sigmoid(v):
    return 1.0 / (1.0 + np.exp(-np.maximum(v, -700.0)))


K, T, S, D, H, V, Z, W = 512, 2048, 512, 2, 512, 256, 512, 2048
P = 2 ** 7


def setup_inputs():
    n = np.random.standard_normal
    s = mx_kscale(K)[:, None]
    packed_xT = pack_weight(n((K, T)) * s)
    packed_eT = pack_weight(n((K, W)) * s)
    return {
        "x_words": packed_xT[0],
        "x_scales": packed_xT[1],
        "w1": (n((K, H)) / np.sqrt(K) / s).astype(np.float32),
        "w2": (n((K, H)) / np.sqrt(K) / s).astype(np.float32),
        "e_words": packed_eT[0],
        "e_scales": packed_eT[1],
        "unit": (np.random.uniform(0.6, 1.4, (K, 1)) / np.sqrt(K) / s).astype(np.float32),
        "acc_": (np.tile(np.random.uniform(0.2, 1.0, W), (P, 1))).astype(np.float32),
        "offs": striped(np.random.permutation(T)[:S]),
        "site": striped(np.random.permutation(W)[:Z]),
        "alt": striped(np.random.permutation(V)),
    }


def reference(x_words, x_scales, w1, w2, e_words, e_scales, unit, acc_, offs, site, alt):
    xq = unpack_weight(x_words, x_scales)[:, unstriped(offs)]
    y = mxq(f64(w1), 0, "e4m3").T @ xq
    yw = mxq(f64(w2), 0, "e4m3").T @ xq
    pm = relu(y) * sigmoid(yw)
    guide = pm.reshape(len(pm), -1, D).sum(axis=2)
    gd = guide - (0.5 * guide[:, unstriped(alt)])
    hid = f64(unit) * gd
    e_site = unpack_weight(e_words, e_scales)[:, unstriped(site)]
    sc = mxq(hid, 0, "e4m3").T @ e_site
    cut_ = sigmoid(2.0 * sc) * (f64(acc_)[:1][:, unstriped(site)])
    offt = cut_.sum(axis=1, keepdims=True)
    return 100.0 * (cut_ / (offt + 1.0))

@@ -1,0 +1,179 @@
+from contextlib import ExitStack
+
+import concourse.mybir as mybir
+
+K, T, S, H, V, Z, W = 512, 2048, 512, 512, 256, 512, 2048
+FLOPS = 2 * K * H * S * 2 + 2 * H * V * Z
+
+F32 = mybir.dt.float32
+BF16 = mybir.dt.bfloat16
+I32 = mybir.dt.int32
+U32 = mybir.dt.uint32
+U16 = mybir.dt.uint16
+U8 = mybir.dt.uint8
+FP8X4 = mybir.dt.float8_e4m3fn_x4
+ALU = mybir.AluOpType
+ACT = mybir.ActivationFunctionType
+
+P = 128
+PACK = 4
+E_ROW = 4
+
+
+def tile_picked_ycrispr_spec_p_kernel(tc, x_words, x_scales, w1, w2, e_words, e_scales, unit, acc_, offs, site, alt, out):
+    nc = tc.nc
+    with ExitStack() as ctx:
+        sb = ctx.enter_context(tc.tile_pool(name="sb", bufs=1))
+        ps = ctx.enter_context(tc.psum_pool(name="ps", bufs=1))
+
+        offs_t = sb.tile([P, S // 16], U16, name="offs_t")
+        site_t = sb.tile([P, Z // 16], U16, name="site_t")
+        alt_t = sb.tile([P, V // 16], U16, name="alt_t")
+        xw = sb.tile([P, T], I32, name="xw", align_bytes=64)
+        ew = sb.tile([P, W], I32, name="ew", align_bytes=64)
+        xs = sb.tile([P, T], U8, name="xs", align_bytes=64)
+        es = sb.tile([P, W], U8, name="es", align_bytes=64)
+        w1_raw = sb.tile([P, PACK, H], F32, name="w1_raw", tag="w1_raw", align_bytes=64)
+        w2_raw = sb.tile([P, PACK, H], F32, name="w2_raw", align_bytes=64)
+        unit_t = sb.tile([P, PACK], F32, name="unit_t")
+        acc_t = sb.tile([P, W], F32, name="acc_t", align_bytes=64)
+
+        def load_words(tile, words):
+            nc.sync.dma_start(out=tile[:], in_=words[0].rearrange("p c r -> p (c r)").bitcast(I32))
+
+        def load_scales(queue, tile, scales, row):
+            for q in range(4):
+                queue.dma_start(
+                    out=tile[32 * q + row : 32 * q + row + 4, :].bitcast(I32),
+                    in_=scales[0, 4 * q : 4 * q + 4, :].bitcast(I32),
+                )
+
+        nc.gpsimd.memset(xs[:].bitcast(I32), 0)
+        nc.gpsimd.memset(es[:].bitcast(I32), 0)
+        load_words(xw, x_words)
+        nc.sync.dma_start(offs_t[:], offs)
+        load_scales(nc.sync, xs, x_scales, 0)
+        nc.sync.dma_start(out=w2_raw[:], in_=w2.rearrange("(p j) c -> p j c", j=PACK))
+        nc.sync.dma_start(site_t[:], site)
+        load_scales(nc.sync, es, e_scales, E_ROW)
+        nc.sync.dma_start(out=w1_raw[:], in_=w1.rearrange("(p j) c -> p j c", j=PACK))
+        load_words(ew, e_words)
+        nc.sync.dma_start(out=unit_t[:], in_=unit.rearrange("(p t) o -> p (t o)", t=PACK))
+        nc.sync.dma_start(alt_t[:], alt)
+        nc.sync.dma_start(out=acc_t[:], in_=acc_)
+
+        xg = sb.tile([P, S], U32, name="xg", align_bytes=64)
+        xsg = sb.tile([P, S], U8, name="xsg", align_bytes=64)
+        esg = sb.tile([P, Z], U8, name="esg", align_bytes=64)
+        nc.vector.tensor_copy(xg[:], xw[:].bitcast(U32).indirect(offs_t[:]))
+        nc.vector.tensor_copy(xsg[:], xs[:].indirect(offs_t[:]))
+
+        def round_weights(raw, name):
+            pairs = []
+            for pair in range(2):
+                grouped = sb.tile([P, 2, P, PACK], BF16, name="%s_bf%d" % (name, pair), align_bytes=64)
+                src = raw[:].rearrange("p j (m t) -> p m j t", t=PACK)[:, :, :, 2 * pair : 2 * pair + 2]
+                dst = grouped[:].rearrange("p t m j -> p m j t")
+                if pair == 0 or name == "w2":
+                    nc.vector.tensor_copy(out=dst, in_=src)
+                else:
+                    nc.scalar.copy(out=dst, in_=src)
+                pairs.append(grouped)
+            return pairs
+
+        def quantise(pairs, t, name):
+            codes = sb.tile([P, P], U32, name="%s_codes%d" % (name, t), align_bytes=64)
+            plane = sb.tile([P, P], U8, name="%s_plane%d" % (name, t), align_bytes=64)
+            nc.vector.quantize_mx(
+                out=codes[:].bitcast(FP8X4),
+                scales=plane[:],
+                in_=pairs[t // 2][:, t % 2, :, :].rearrange("p m j -> p (m j)"),
+            )
+            return codes, plane
+
+        def product(weights, t, name):
+            codes, plane = weights
+            bank = ps.tile([P, S], F32, name="%s_bank%d" % (name, t))
+            nc.tensor.matmul_mx(
+                out=bank[:], lhsT=codes[:].bitcast(FP8X4), lhsT_scale=plane[:],
+                rhs=xg[:].bitcast(FP8X4), rhs_scale=xsg[:], start=True, stop=True,
+            )
+            return bank
+
+        w2_pairs = round_weights(w2_raw, "w2")
+        w2_mx = [quantise(w2_pairs, t, "w2") for t in range(PACK)]
+        nc.vector.tensor_copy(esg[:], es[:].indirect(site_t[:]))
+        w1_pairs = round_weights(w1_raw, "w1")
+        first_gate = sb.tile([P, S], F32, name="first_gate", align_bytes=64)
+        later_gates = sb.tile([P, PACK - 1, S], F32, name="later_gates", tag="w1_raw", align_bytes=64)
+        gates = [first_gate[:]] + [later_gates[:, t, :] for t in range(PACK - 1)]
+        for t in range(PACK):
+            nc.scalar.activation(gates[t], product(w2_mx[t], t, "w2")[:], ACT.Sigmoid)
+        banks = [product(quantise(w1_pairs, t, "w1"), t, "w1") for t in range(PACK)]
+
+        scaled = sb.tile([P, PACK, V], F32, name="scaled", align_bytes=64)
+        rival = [sb.tile([P, PACK, P], F32, name="rival%d" % h, align_bytes=64) for h in range(2)]
+        gated = []
+
+        def gate_tile(t):
+            pm = sb.tile([P, V, 2], F32, name="pm%d" % t, tag="pm%d" % t, align_bytes=64)
+            nc.vector.scalar_tensor_tensor(
+                out=pm[:].rearrange("p v d -> p (v d)"), in0=banks[t][:], scalar=0.0, in1=gates[t],
+                op0=ALU.max, op1=ALU.mult,
+            )
+            gated.append(pm)
+
+        def guide_tile(t):
+            guide = sb.tile([P, V], F32, name="guide%d" % t, tag="guide%d" % t, align_bytes=64)
+            nc.vector.tensor_tensor(guide[:], gated[t][:, :, 0], gated[t][:, :, 1], ALU.add)
+            nc.gpsimd.tensor_scalar(scaled[:, t, :], guide[:], unit_t[:, t : t + 1], 0.0, ALU.mult, ALU.add)
+            for h in range(2):
+                nc.scalar.activation(
+                    rival[h][:, t, :], scaled[:, t, :].indirect(alt_t[:, 8 * h : 8 * h + 8]), ACT.Copy, scale=-0.5
+                )
+
+        gate_tile(0)
+        for t in range(1, PACK):
+            gate_tile(t)
+            guide_tile(t - 1)
+        guide_tile(PACK - 1)
+
+        eg = sb.tile([P, Z], U32, name="eg", tag="pm3", align_bytes=64)
+        nc.vector.tensor_copy(eg[:], ew[:].bitcast(U32).indirect(site_t[:]))
+
+        openness = sb.tile([P, Z + 1], F32, name="openness", tag="guide3", align_bytes=64)
+        nc.gpsimd.memset(openness[:, Z : Z + 1], 1.0)
+        nc.scalar.activation(openness[:, 0:Z], acc_t[:].indirect(site_t[:]), ACT.Copy)
+
+        hid = []
+        for h in range(2):
+            rounded = sb.tile([P, P, PACK], BF16, name="hid%d" % h, align_bytes=64)
+            nc.vector.tensor_tensor(
+                rounded[:].rearrange("p (c i) t -> p c t i", i=4),
+                scaled[:, :, P * h : P * h + P].rearrange("p t (c i) -> p c t i", i=4),
+                rival[h][:].rearrange("p t (c i) -> p c t i", i=4),
+                ALU.add,
+            )
+            hid.append(rounded)
+        for h in range(2):
+            codes = sb.tile([P, P], U32, name="hid_codes%d" % h, align_bytes=64)
+            plane = sb.tile([P, P], U8, name="hid_plane%d" % h, align_bytes=64)
+            nc.vector.quantize_mx(out=codes[:].bitcast(FP8X4), scales=plane[:], in_=hid[h][:].rearrange("p v t -> p (v t)"))
+            bank = ps.tile([P, Z], F32, name="w2_bank%d" % h)
+            nc.tensor.matmul_mx(
+                out=bank[:], lhsT=codes[:].bitcast(FP8X4), lhsT_scale=plane[:],
+                rhs=eg[:].bitcast(FP8X4), rhs_scale=esg[E_ROW:P, :], start=True, stop=True,
+            )
+            sig = sb.tile([P, Z + 1], F32, name="sig%d" % h, align_bytes=64)
+            nc.gpsimd.memset(sig[:, Z : Z + 1], 1.0)
+            nc.scalar.activation(sig[:, 0:Z], bank[:], ACT.Sigmoid, scale=2.0)
+            cut = sb.tile([P, Z + 1], F32, name="cut%d" % h, align_bytes=64)
+            total = sb.tile([P, 1], F32, name="total%d" % h)
+            nc.vector.scalar_tensor_tensor(
+                out=cut[:], in0=sig[:], scalar=1.0, in1=openness[:], op0=ALU.mult, op1=ALU.mult, accum_out=total[:]
+            )
+            inverse = sb.tile([P, 1], F32, name="inverse%d" % h)
+            nc.vector.reciprocal(inverse[:], total[:])
+            result = sb.tile([P, Z], F32, name="result%d" % h, align_bytes=64)
+            nc.vector.tensor_scalar(result[:], cut[:, 0:Z], inverse[:], 100.0, ALU.mult, ALU.mult)
+            nc.sync.dma_start(out=out[P * h : P * h + P, :], in_=result[:])

@@ -42,10 +42,10 @@ def tile_picked_ycrispr_spec_p_kernel(tc, x_words, x_scales, w1, w2, e_words, e_
             nc.sync.dma_start(out=tile[:], in_=words[0].rearrange("p c r -> p (c r)").bitcast(I32))
 
         def load_scales(queue, tile, scales, row):
-            for q in range(4):
+            for r in range(4):
                 queue.dma_start(
-                    out=tile[32 * q + row : 32 * q + row + 4, :].bitcast(I32),
-                    in_=scales[0, 4 * q : 4 * q + 4, :].bitcast(I32),
+                    out=tile[row + r : P : 32, :].bitcast(I32),
+                    in_=scales[0, r:16:4, :].bitcast(I32),
                 )
 
         nc.gpsimd.memset(xs[:].bitcast(I32), 0)

@@ -81,27 +81,27 @@ def tile_picked_ycrispr_spec_p_kernel(tc, x_words, x_scales, w1, w2, e_words, e_
                 pairs.append(grouped)
             return pairs
 
-        def quantise(pairs, t, name):
-            codes = sb.tile([P, P], U32, name="%s_codes%d" % (name, t), align_bytes=64)
-            plane = sb.tile([P, P], U8, name="%s_plane%d" % (name, t), align_bytes=64)
+        def quantise(grouped, first, count, name):
+            codes = sb.tile([P, count, P], U32, name="%s_codes" % name, align_bytes=64)
+            plane = sb.tile([P, count, P], U8, name="%s_plane" % name, align_bytes=64)
             nc.vector.quantize_mx(
-                out=codes[:].bitcast(FP8X4),
-                scales=plane[:],
-                in_=pairs[t // 2][:, t % 2, :, :].rearrange("p m j -> p (m j)"),
+                out=codes[:].rearrange("p t m -> p (t m)").bitcast(FP8X4),
+                scales=plane[:].rearrange("p t m -> p (t m)"),
+                in_=grouped[:, first : first + count, :, :].rearrange("p t m j -> p (t m j)"),
             )
-            return codes, plane
+            return [(codes[:, i, :], plane[:, i, :]) for i in range(count)]
 
         def product(weights, t, name):
             codes, plane = weights
             bank = ps.tile([P, S], F32, name="%s_bank%d" % (name, t))
             nc.tensor.matmul_mx(
-                out=bank[:], lhsT=codes[:].bitcast(FP8X4), lhsT_scale=plane[:],
+                out=bank[:], lhsT=codes.bitcast(FP8X4), lhsT_scale=plane,
                 rhs=xg[:].bitcast(FP8X4), rhs_scale=xsg[:], start=True, stop=True,
             )
             return bank
 
         w2_pairs = round_weights(w2_raw, "w2")
-        w2_mx = [quantise(w2_pairs, t, "w2") for t in range(PACK)]
+        w2_mx = quantise(w2_pairs[0], 0, 2, "w2_low") + quantise(w2_pairs[1], 0, 2, "w2_high")
         nc.vector.tensor_copy(esg[:], es[:].indirect(site_t[:]))
         w1_pairs = round_weights(w1_raw, "w1")
         first_gate = sb.tile([P, S], F32, name="first_gate", align_bytes=64)
@@ -109,10 +109,12 @@ def tile_picked_ycrispr_spec_p_kernel(tc, x_words, x_scales, w1, w2, e_words, e_
         gates = [first_gate[:]] + [later_gates[:, t, :] for t in range(PACK - 1)]
         for t in range(PACK):
             nc.scalar.activation(gates[t], product(w2_mx[t], t, "w2")[:], ACT.Sigmoid)
-        banks = [product(quantise(w1_pairs, t, "w1"), t, "w1") for t in range(PACK)]
+        w1_mx = quantise(w1_pairs[0], 0, 1, "w1_first") + quantise(w1_pairs[0], 1, 1, "w1_second")
+        w1_mx = w1_mx + quantise(w1_pairs[1], 0, 2, "w1_high")
+        banks = [product(w1_mx[t], t, "w1") for t in range(PACK)]
 
         scaled = sb.tile([P, PACK, V], F32, name="scaled", align_bytes=64)
-        rival = [sb.tile([P, PACK, P], F32, name="rival%d" % h, align_bytes=64) for h in range(2)]
+        rival = [sb.tile([P, PACK, P], F32, name="rival%d" % h, tag="rival%d" % h, align_bytes=64) for h in range(2)]
         gated = []
 
         def gate_tile(t):
@@ -126,7 +128,10 @@ def tile_picked_ycrispr_spec_p_kernel(tc, x_words, x_scales, w1, w2, e_words, e_
         def guide_tile(t):
             guide = sb.tile([P, V], F32, name="guide%d" % t, tag="guide%d" % t, align_bytes=64)
             nc.vector.tensor_tensor(guide[:], gated[t][:, :, 0], gated[t][:, :, 1], ALU.add)
-            nc.gpsimd.tensor_scalar(scaled[:, t, :], guide[:], unit_t[:, t : t + 1], 0.0, ALU.mult, ALU.add)
+            if t < 2:
+                nc.scalar.activation(scaled[:, t, :], guide[:], ACT.Copy, scale=unit_t[:, t : t + 1])
+            else:
+                nc.vector.tensor_scalar(scaled[:, t, :], guide[:], unit_t[:, t : t + 1], None, ALU.mult)
             for h in range(2):
                 nc.scalar.activation(
                     rival[h][:, t, :], scaled[:, t, :].indirect(alt_t[:, 8 * h : 8 * h + 8]), ACT.Copy, scale=-0.5
@@ -138,12 +143,8 @@ def tile_picked_ycrispr_spec_p_kernel(tc, x_words, x_scales, w1, w2, e_words, e_
             guide_tile(t - 1)
         guide_tile(PACK - 1)
 
-        eg = sb.tile([P, Z], U32, name="eg", tag="pm3", align_bytes=64)
+        eg = sb.tile([P, Z], U32, name="eg", tag="guide3", align_bytes=64)
         nc.vector.tensor_copy(eg[:], ew[:].bitcast(U32).indirect(site_t[:]))
-
-        openness = sb.tile([P, Z + 1], F32, name="openness", tag="guide3", align_bytes=64)
-        nc.gpsimd.memset(openness[:, Z : Z + 1], 1.0)
-        nc.scalar.activation(openness[:, 0:Z], acc_t[:].indirect(site_t[:]), ACT.Copy)
 
         hid = []
         for h in range(2):
@@ -155,18 +156,25 @@ def tile_picked_ycrispr_spec_p_kernel(tc, x_words, x_scales, w1, w2, e_words, e_
                 ALU.add,
             )
             hid.append(rounded)
+
+        openness = sb.tile([P, Z + 1], F32, name="openness", tag="rival0", align_bytes=64)
+        nc.gpsimd.memset(openness[:, Z : Z + 1], 1.0)
+        nc.scalar.activation(openness[:, 0:Z], acc_t[:].indirect(site_t[:]), ACT.Copy)
+
         for h in range(2):
             codes = sb.tile([P, P], U32, name="hid_codes%d" % h, align_bytes=64)
             plane = sb.tile([P, P], U8, name="hid_plane%d" % h, align_bytes=64)
             nc.vector.quantize_mx(out=codes[:].bitcast(FP8X4), scales=plane[:], in_=hid[h][:].rearrange("p v t -> p (v t)"))
-            bank = ps.tile([P, Z], F32, name="w2_bank%d" % h)
-            nc.tensor.matmul_mx(
-                out=bank[:], lhsT=codes[:].bitcast(FP8X4), lhsT_scale=plane[:],
-                rhs=eg[:].bitcast(FP8X4), rhs_scale=esg[E_ROW:P, :], start=True, stop=True,
-            )
             sig = sb.tile([P, Z + 1], F32, name="sig%d" % h, align_bytes=64)
             nc.gpsimd.memset(sig[:, Z : Z + 1], 1.0)
-            nc.scalar.activation(sig[:, 0:Z], bank[:], ACT.Sigmoid, scale=2.0)
+            for part in range(2):
+                cols = slice(part * Z // 2, (part + 1) * Z // 2)
+                bank = ps.tile([P, Z // 2], F32, name="w2_bank%d" % (2 * h + part))
+                nc.tensor.matmul_mx(
+                    out=bank[:], lhsT=codes[:].bitcast(FP8X4), lhsT_scale=plane[:],
+                    rhs=eg[:, cols].bitcast(FP8X4), rhs_scale=esg[E_ROW:P, cols], start=True, stop=True,
+                )
+                nc.scalar.activation(sig[:, cols], bank[:], ACT.Sigmoid, scale=2.0)
             cut = sb.tile([P, Z + 1], F32, name="cut%d" % h, align_bytes=64)
             total = sb.tile([P, 1], F32, name="total%d" % h)
             nc.vector.scalar_tensor_tensor(

@@ -18,6 +18,9 @@ ACT = mybir.ActivationFunctionType
 P = 128
 PACK = 4
 E_ROW = 4
+HALF = Z // 2
+LEAD = 4
+WIDE = LEAD + Z + 1
 
 
 def tile_picked_ycrispr_spec_p_kernel(tc, x_words, x_scales, w1, w2, e_words, e_scales, unit, acc_, offs, site, alt, out):
@@ -48,6 +51,10 @@ def tile_picked_ycrispr_spec_p_kernel(tc, x_words, x_scales, w1, w2, e_words, e_
                     in_=scales[0, r:16:4, :].bitcast(I32),
                 )
 
+        warm_in = sb.tile([P, 1], F32, name="warm_in")
+        warm_out = sb.tile([P, 1], F32, name="warm_out")
+        nc.vector.memset(warm_in[:], 0.0)
+        nc.scalar.activation(warm_out[:], warm_in[:], ACT.Sigmoid)
         nc.gpsimd.memset(xs[:].bitcast(I32), 0)
         nc.gpsimd.memset(es[:].bitcast(I32), 0)
         load_words(xw, x_words)
@@ -74,7 +81,7 @@ def tile_picked_ycrispr_spec_p_kernel(tc, x_words, x_scales, w1, w2, e_words, e_
                 grouped = sb.tile([P, 2, P, PACK], BF16, name="%s_bf%d" % (name, pair), align_bytes=64)
                 src = raw[:].rearrange("p j (m t) -> p m j t", t=PACK)[:, :, :, 2 * pair : 2 * pair + 2]
                 dst = grouped[:].rearrange("p t m j -> p m j t")
-                if pair == 0 or name == "w2":
+                if pair == 0:
                     nc.vector.tensor_copy(out=dst, in_=src)
                 else:
                     nc.scalar.copy(out=dst, in_=src)
@@ -128,7 +135,7 @@ def tile_picked_ycrispr_spec_p_kernel(tc, x_words, x_scales, w1, w2, e_words, e_
         def guide_tile(t):
             guide = sb.tile([P, V], F32, name="guide%d" % t, tag="guide%d" % t, align_bytes=64)
             nc.vector.tensor_tensor(guide[:], gated[t][:, :, 0], gated[t][:, :, 1], ALU.add)
-            if t < 2:
+            if t < 1:
                 nc.scalar.activation(scaled[:, t, :], guide[:], ACT.Copy, scale=unit_t[:, t : t + 1])
             else:
                 nc.vector.tensor_scalar(scaled[:, t, :], guide[:], unit_t[:, t : t + 1], None, ALU.mult)
@@ -143,12 +150,16 @@ def tile_picked_ycrispr_spec_p_kernel(tc, x_words, x_scales, w1, w2, e_words, e_
             guide_tile(t - 1)
         guide_tile(PACK - 1)
 
-        eg = sb.tile([P, Z], U32, name="eg", tag="guide3", align_bytes=64)
-        nc.vector.tensor_copy(eg[:], ew[:].bitcast(U32).indirect(site_t[:]))
+        def pick_sites(part, tag):
+            words = sb.tile([P, HALF], U32, name="eg%d" % part, tag=tag, align_bytes=64)
+            nc.vector.tensor_copy(words[:], ew[:].bitcast(U32).indirect(site_t[:, 16 * part : 16 * part + 16]))
+            return words
+
+        eg = [pick_sites(0, "guide3")]
 
         hid = []
         for h in range(2):
-            rounded = sb.tile([P, P, PACK], BF16, name="hid%d" % h, align_bytes=64)
+            rounded = sb.tile([P, P, PACK], BF16, name="hid%d" % h, tag="hid%d" % h, align_bytes=64)
             nc.vector.tensor_tensor(
                 rounded[:].rearrange("p (c i) t -> p c t i", i=4),
                 scaled[:, :, P * h : P * h + P].rearrange("p t (c i) -> p c t i", i=4),
@@ -157,31 +168,43 @@ def tile_picked_ycrispr_spec_p_kernel(tc, x_words, x_scales, w1, w2, e_words, e_
             )
             hid.append(rounded)
 
-        openness = sb.tile([P, Z + 1], F32, name="openness", tag="rival0", align_bytes=64)
-        nc.gpsimd.memset(openness[:, Z : Z + 1], 1.0)
-        nc.scalar.activation(openness[:, 0:Z], acc_t[:].indirect(site_t[:]), ACT.Copy)
+        openness = sb.tile([P, WIDE], F32, name="openness", tag="rival0", align_bytes=64)
+        nc.gpsimd.memset(openness[:, LEAD - 1 : WIDE : Z + 1], 1.0)
+        nc.scalar.activation(openness[:, LEAD : LEAD + Z], acc_t[:].indirect(site_t[:]), ACT.Copy)
 
+        hid_mx = []
         for h in range(2):
             codes = sb.tile([P, P], U32, name="hid_codes%d" % h, align_bytes=64)
             plane = sb.tile([P, P], U8, name="hid_plane%d" % h, align_bytes=64)
             nc.vector.quantize_mx(out=codes[:].bitcast(FP8X4), scales=plane[:], in_=hid[h][:].rearrange("p v t -> p (v t)"))
-            sig = sb.tile([P, Z + 1], F32, name="sig%d" % h, align_bytes=64)
-            nc.gpsimd.memset(sig[:, Z : Z + 1], 1.0)
-            for part in range(2):
-                cols = slice(part * Z // 2, (part + 1) * Z // 2)
-                bank = ps.tile([P, Z // 2], F32, name="w2_bank%d" % (2 * h + part))
+            hid_mx.append((codes, plane))
+        eg.append(pick_sites(1, "hid1"))
+
+        sig = [sb.tile([P, WIDE], F32, name="sig%d" % h, align_bytes=64) for h in range(2)]
+        cut = [sb.tile([P, WIDE], F32, name="cut%d" % h, align_bytes=64) for h in range(2)]
+        total = [sb.tile([P, 1], F32, name="total%d" % h) for h in range(2)]
+        for h in range(2):
+            nc.gpsimd.memset(sig[h][:, LEAD - 1 : LEAD], 1.0)
+        for part in range(2):
+            for h in range(2):
+                codes, plane = hid_mx[h]
+                bank = ps.tile([P, HALF], F32, name="w2_bank%d" % (2 * part + h))
                 nc.tensor.matmul_mx(
                     out=bank[:], lhsT=codes[:].bitcast(FP8X4), lhsT_scale=plane[:],
-                    rhs=eg[:, cols].bitcast(FP8X4), rhs_scale=esg[E_ROW:P, cols], start=True, stop=True,
+                    rhs=eg[part][:].bitcast(FP8X4), rhs_scale=esg[E_ROW:P, part * HALF : (part + 1) * HALF],
+                    start=True, stop=True,
                 )
-                nc.scalar.activation(sig[:, cols], bank[:], ACT.Sigmoid, scale=2.0)
-            cut = sb.tile([P, Z + 1], F32, name="cut%d" % h, align_bytes=64)
-            total = sb.tile([P, 1], F32, name="total%d" % h)
-            nc.vector.scalar_tensor_tensor(
-                out=cut[:], in0=sig[:], scalar=1.0, in1=openness[:], op0=ALU.mult, op1=ALU.mult, accum_out=total[:]
-            )
+                first = LEAD + part * HALF
+                nc.scalar.activation(sig[h][:, first : first + HALF], bank[:], ACT.Sigmoid, scale=2.0)
+                cols = slice(LEAD - 1, first + HALF) if part == 0 else slice(first, WIDE)
+                nc.vector.scalar_tensor_tensor(
+                    out=cut[h][:, cols], in0=sig[h][:, cols], scalar=1.0, in1=openness[:, cols],
+                    op0=ALU.mult, op1=ALU.mult,
+                    accum_out=sig[h][:, WIDE - 1 : WIDE] if part == 0 else total[h][:],
+                )
+        for h in range(2):
             inverse = sb.tile([P, 1], F32, name="inverse%d" % h)
-            nc.vector.reciprocal(inverse[:], total[:])
+            nc.vector.reciprocal(inverse[:], total[h][:])
             result = sb.tile([P, Z], F32, name="result%d" % h, align_bytes=64)
-            nc.vector.tensor_scalar(result[:], cut[:, 0:Z], inverse[:], 100.0, ALU.mult, ALU.mult)
+            nc.vector.tensor_scalar(result[:], cut[h][:, LEAD : LEAD + Z], inverse[:], 100.0, ALU.mult, ALU.mult)
             nc.sync.dma_start(out=out[P * h : P * h + P, :], in_=result[:])

@@ -51,10 +51,6 @@ def tile_picked_ycrispr_spec_p_kernel(tc, x_words, x_scales, w1, w2, e_words, e_
                     in_=scales[0, r:16:4, :].bitcast(I32),
                 )
 
-        warm_in = sb.tile([P, 1], F32, name="warm_in")
-        warm_out = sb.tile([P, 1], F32, name="warm_out")
-        nc.vector.memset(warm_in[:], 0.0)
-        nc.scalar.activation(warm_out[:], warm_in[:], ACT.Sigmoid)
         nc.gpsimd.memset(xs[:].bitcast(I32), 0)
         nc.gpsimd.memset(es[:].bitcast(I32), 0)
         load_words(xw, x_words)
@@ -64,9 +60,9 @@ def tile_picked_ycrispr_spec_p_kernel(tc, x_words, x_scales, w1, w2, e_words, e_
         nc.sync.dma_start(site_t[:], site)
         load_scales(nc.sync, es, e_scales, E_ROW)
         nc.sync.dma_start(out=w1_raw[:], in_=w1.rearrange("(p j) c -> p j c", j=PACK))
-        load_words(ew, e_words)
-        nc.sync.dma_start(out=unit_t[:], in_=unit.rearrange("(p t) o -> p (t o)", t=PACK))
         nc.sync.dma_start(alt_t[:], alt)
+        nc.sync.dma_start(out=unit_t[:], in_=unit.rearrange("(p t) o -> p (t o)", t=PACK))
+        load_words(ew, e_words)
         nc.sync.dma_start(out=acc_t[:], in_=acc_)
 
         xg = sb.tile([P, S], U32, name="xg", align_bytes=64)
@@ -81,7 +77,7 @@ def tile_picked_ycrispr_spec_p_kernel(tc, x_words, x_scales, w1, w2, e_words, e_
                 grouped = sb.tile([P, 2, P, PACK], BF16, name="%s_bf%d" % (name, pair), align_bytes=64)
                 src = raw[:].rearrange("p j (m t) -> p m j t", t=PACK)[:, :, :, 2 * pair : 2 * pair + 2]
                 dst = grouped[:].rearrange("p t m j -> p m j t")
-                if pair == 0:
+                if pair == 0 or name == "w2":
                     nc.vector.tensor_copy(out=dst, in_=src)
                 else:
                     nc.scalar.copy(out=dst, in_=src)
@@ -169,7 +165,9 @@ def tile_picked_ycrispr_spec_p_kernel(tc, x_words, x_scales, w1, w2, e_words, e_
             hid.append(rounded)
 
         openness = sb.tile([P, WIDE], F32, name="openness", tag="rival0", align_bytes=64)
-        nc.gpsimd.memset(openness[:, LEAD - 1 : WIDE : Z + 1], 1.0)
+        ones = sb.tile([P, 2], F32, name="ones")
+        nc.gpsimd.memset(ones[:], 1.0)
+        nc.scalar.copy(out=openness[:, LEAD - 1 : WIDE : Z + 1], in_=ones[:])
         nc.scalar.activation(openness[:, LEAD : LEAD + Z], acc_t[:].indirect(site_t[:]), ACT.Copy)
 
         hid_mx = []

from contextlib import ExitStack

import concourse.mybir as mybir

K, T, S, H, V, Z, W = 512, 2048, 512, 512, 256, 512, 2048
FLOPS = 2 * K * H * S * 2 + 2 * H * V * Z

F32 = mybir.dt.float32
BF16 = mybir.dt.bfloat16
I32 = mybir.dt.int32
U32 = mybir.dt.uint32
U16 = mybir.dt.uint16
U8 = mybir.dt.uint8
FP8X4 = mybir.dt.float8_e4m3fn_x4
ALU = mybir.AluOpType
ACT = mybir.ActivationFunctionType

P = 128
PACK = 4
E_ROW = 4
HALF = Z // 2
LEAD = 4
WIDE = LEAD + Z + 1


def tile_picked_ycrispr_spec_p_kernel(tc, x_words, x_scales, w1, w2, e_words, e_scales, unit, acc_, offs, site, alt, out):
    nc = tc.nc
    with ExitStack() as ctx:
        sb = ctx.enter_context(tc.tile_pool(name="sb", bufs=1))
        ps = ctx.enter_context(tc.psum_pool(name="ps", bufs=1))

        offs_t = sb.tile([P, S // 16], U16, name="offs_t")
        site_t = sb.tile([P, Z // 16], U16, name="site_t")
        alt_t = sb.tile([P, V // 16], U16, name="alt_t")
        xw = sb.tile([P, T], I32, name="xw", align_bytes=64)
        ew = sb.tile([P, W], I32, name="ew", align_bytes=64)
        xs = sb.tile([P, T], U8, name="xs", align_bytes=64)
        es = sb.tile([P, W], U8, name="es", align_bytes=64)
        w1_raw = sb.tile([P, PACK, H], F32, name="w1_raw", tag="w1_raw", align_bytes=64)
        w2_raw = sb.tile([P, PACK, H], F32, name="w2_raw", align_bytes=64)
        unit_t = sb.tile([P, PACK], F32, name="unit_t")
        acc_t = sb.tile([P, W], F32, name="acc_t", align_bytes=64)

        def load_words(tile, words):
            nc.sync.dma_start(out=tile[:], in_=words[0].rearrange("p c r -> p (c r)").bitcast(I32))

        def load_scales(queue, tile, scales, row):
            for r in range(4):
                queue.dma_start(
                    out=tile[row + r : P : 32, :].bitcast(I32),
                    in_=scales[0, r:16:4, :].bitcast(I32),
                )

        nc.gpsimd.memset(xs[:].bitcast(I32), 0)
        nc.gpsimd.memset(es[:].bitcast(I32), 0)
        load_words(xw, x_words)
        nc.sync.dma_start(offs_t[:], offs)
        load_scales(nc.sync, xs, x_scales, 0)
        nc.sync.dma_start(out=w2_raw[:], in_=w2.rearrange("(p j) c -> p j c", j=PACK))
        nc.sync.dma_start(site_t[:], site)
        load_scales(nc.sync, es, e_scales, E_ROW)
        nc.sync.dma_start(out=w1_raw[:], in_=w1.rearrange("(p j) c -> p j c", j=PACK))
        nc.sync.dma_start(alt_t[:], alt)
        nc.sync.dma_start(out=unit_t[:], in_=unit.rearrange("(p t) o -> p (t o)", t=PACK))
        load_words(ew, e_words)
        nc.sync.dma_start(out=acc_t[:], in_=acc_)

        xg = sb.tile([P, S], U32, name="xg", align_bytes=64)
        xsg = sb.tile([P, S], U8, name="xsg", align_bytes=64)
        esg = sb.tile([P, Z], U8, name="esg", align_bytes=64)
        nc.vector.tensor_copy(xg[:], xw[:].bitcast(U32).indirect(offs_t[:]))
        nc.vector.tensor_copy(xsg[:], xs[:].indirect(offs_t[:]))

        def round_weights(raw, name):
            pairs = []
            for pair in range(2):
                grouped = sb.tile([P, 2, P, PACK], BF16, name="%s_bf%d" % (name, pair), align_bytes=64)
                src = raw[:].rearrange("p j (m t) -> p m j t", t=PACK)[:, :, :, 2 * pair : 2 * pair + 2]
                dst = grouped[:].rearrange("p t m j -> p m j t")
                if pair == 0 or name == "w2":
                    nc.vector.tensor_copy(out=dst, in_=src)
                else:
                    nc.scalar.copy(out=dst, in_=src)
                pairs.append(grouped)
            return pairs

        def quantise(grouped, first, count, name):
            codes = sb.tile([P, count, P], U32, name="%s_codes" % name, align_bytes=64)
            plane = sb.tile([P, count, P], U8, name="%s_plane" % name, align_bytes=64)
            nc.vector.quantize_mx(
                out=codes[:].rearrange("p t m -> p (t m)").bitcast(FP8X4),
                scales=plane[:].rearrange("p t m -> p (t m)"),
                in_=grouped[:, first : first + count, :, :].rearrange("p t m j -> p (t m j)"),
            )
            return [(codes[:, i, :], plane[:, i, :]) for i in range(count)]

        def product(weights, t, name):
            codes, plane = weights
            bank = ps.tile([P, S], F32, name="%s_bank%d" % (name, t))
            nc.tensor.matmul_mx(
                out=bank[:], lhsT=codes.bitcast(FP8X4), lhsT_scale=plane,
                rhs=xg[:].bitcast(FP8X4), rhs_scale=xsg[:], start=True, stop=True,
            )
            return bank

        w2_pairs = round_weights(w2_raw, "w2")
        w2_mx = quantise(w2_pairs[0], 0, 2, "w2_low") + quantise(w2_pairs[1], 0, 2, "w2_high")
        nc.vector.tensor_copy(esg[:], es[:].indirect(site_t[:]))
        w1_pairs = round_weights(w1_raw, "w1")
        first_gate = sb.tile([P, S], F32, name="first_gate", align_bytes=64)
        later_gates = sb.tile([P, PACK - 1, S], F32, name="later_gates", tag="w1_raw", align_bytes=64)
        gates = [first_gate[:]] + [later_gates[:, t, :] for t in range(PACK - 1)]
        for t in range(PACK):
            nc.scalar.activation(gates[t], product(w2_mx[t], t, "w2")[:], ACT.Sigmoid)
        w1_mx = quantise(w1_pairs[0], 0, 1, "w1_first") + quantise(w1_pairs[0], 1, 1, "w1_second")
        w1_mx = w1_mx + quantise(w1_pairs[1], 0, 2, "w1_high")
        banks = [product(w1_mx[t], t, "w1") for t in range(PACK)]

        scaled = sb.tile([P, PACK, V], F32, name="scaled", align_bytes=64)
        rival = [sb.tile([P, PACK, P], F32, name="rival%d" % h, tag="rival%d" % h, align_bytes=64) for h in range(2)]
        gated = []

        def gate_tile(t):
            pm = sb.tile([P, V, 2], F32, name="pm%d" % t, tag="pm%d" % t, align_bytes=64)
            nc.vector.scalar_tensor_tensor(
                out=pm[:].rearrange("p v d -> p (v d)"), in0=banks[t][:], scalar=0.0, in1=gates[t],
                op0=ALU.max, op1=ALU.mult,
            )
            gated.append(pm)

        def guide_tile(t):
            guide = sb.tile([P, V], F32, name="guide%d" % t, tag="guide%d" % t, align_bytes=64)
            nc.vector.tensor_tensor(guide[:], gated[t][:, :, 0], gated[t][:, :, 1], ALU.add)
            if t < 1:
                nc.scalar.activation(scaled[:, t, :], guide[:], ACT.Copy, scale=unit_t[:, t : t + 1])
            else:
                nc.vector.tensor_scalar(scaled[:, t, :], guide[:], unit_t[:, t : t + 1], None, ALU.mult)
            for h in range(2):
                nc.scalar.activation(
                    rival[h][:, t, :], scaled[:, t, :].indirect(alt_t[:, 8 * h : 8 * h + 8]), ACT.Copy, scale=-0.5
                )

        gate_tile(0)
        for t in range(1, PACK):
            gate_tile(t)
            guide_tile(t - 1)
        guide_tile(PACK - 1)

        def pick_sites(part, tag):
            words = sb.tile([P, HALF], U32, name="eg%d" % part, tag=tag, align_bytes=64)
            nc.vector.tensor_copy(words[:], ew[:].bitcast(U32).indirect(site_t[:, 16 * part : 16 * part + 16]))
            return words

        eg = [pick_sites(0, "guide3")]

        hid = []
        for h in range(2):
            rounded = sb.tile([P, P, PACK], BF16, name="hid%d" % h, tag="hid%d" % h, align_bytes=64)
            nc.vector.tensor_tensor(
                rounded[:].rearrange("p (c i) t -> p c t i", i=4),
                scaled[:, :, P * h : P * h + P].rearrange("p t (c i) -> p c t i", i=4),
                rival[h][:].rearrange("p t (c i) -> p c t i", i=4),
                ALU.add,
            )
            hid.append(rounded)

        openness = sb.tile([P, WIDE], F32, name="openness", tag="rival0", align_bytes=64)
        ones = sb.tile([P, 2], F32, name="ones")
        nc.gpsimd.memset(ones[:], 1.0)
        nc.scalar.copy(out=openness[:, LEAD - 1 : WIDE : Z + 1], in_=ones[:])
        nc.scalar.activation(openness[:, LEAD : LEAD + Z], acc_t[:].indirect(site_t[:]), ACT.Copy)

        hid_mx = []
        for h in range(2):
            codes = sb.tile([P, P], U32, name="hid_codes%d" % h, align_bytes=64)
            plane = sb.tile([P, P], U8, name="hid_plane%d" % h, align_bytes=64)
            nc.vector.quantize_mx(out=codes[:].bitcast(FP8X4), scales=plane[:], in_=hid[h][:].rearrange("p v t -> p (v t)"))
            hid_mx.append((codes, plane))
        eg.append(pick_sites(1, "hid1"))

        sig = [sb.tile([P, WIDE], F32, name="sig%d" % h, align_bytes=64) for h in range(2)]
        cut = [sb.tile([P, WIDE], F32, name="cut%d" % h, align_bytes=64) for h in range(2)]
        total = [sb.tile([P, 1], F32, name="total%d" % h) for h in range(2)]
        for h in range(2):
            nc.gpsimd.memset(sig[h][:, LEAD - 1 : LEAD], 1.0)
        for part in range(2):
            for h in range(2):
                codes, plane = hid_mx[h]
                bank = ps.tile([P, HALF], F32, name="w2_bank%d" % (2 * part + h))
                nc.tensor.matmul_mx(
                    out=bank[:], lhsT=codes[:].bitcast(FP8X4), lhsT_scale=plane[:],
                    rhs=eg[part][:].bitcast(FP8X4), rhs_scale=esg[E_ROW:P, part * HALF : (part + 1) * HALF],
                    start=True, stop=True,
                )
                first = LEAD + part * HALF
                nc.scalar.activation(sig[h][:, first : first + HALF], bank[:], ACT.Sigmoid, scale=2.0)
                cols = slice(LEAD - 1, first + HALF) if part == 0 else slice(first, WIDE)
                nc.vector.scalar_tensor_tensor(
                    out=cut[h][:, cols], in0=sig[h][:, cols], scalar=1.0, in1=openness[:, cols],
                    op0=ALU.mult, op1=ALU.mult,
                    accum_out=sig[h][:, WIDE - 1 : WIDE] if part == 0 else total[h][:],
                )
        for h in range(2):
            inverse = sb.tile([P, 1], F32, name="inverse%d" % h)
            nc.vector.reciprocal(inverse[:], total[h][:])
            result = sb.tile([P, Z], F32, name="result%d" % h, align_bytes=64)
            nc.vector.tensor_scalar(result[:], cut[h][:, LEAD : LEAD + Z], inverse[:], 100.0, ALU.mult, ALU.mult)
            nc.sync.dma_start(out=out[P * h : P * h + P, :], in_=result[:])
